import numpy as np
import ml_dtypes


def mxq(x, axis, fmt="e4m3"):
    dtype, down = {"e4m3": (ml_dtypes.float8_e4m3fn, 7), "e5m2": (ml_dtypes.float8_e5m2, 14)}[fmt]
    v = np.moveaxis(np.asarray(x, np.float32).astype(ml_dtypes.bfloat16).astype(np.float64), axis, -1)
    blocks = v.reshape(v.shape[:-1] + (-1, 32))
    amax = np.abs(blocks).max(-1, keepdims=True)
    byte = np.maximum(np.where(amax > 0, np.frexp(amax)[1] - 1 + 127, 0) - down, 1)
    scale = np.exp2(byte - 127.0)
    codes = (blocks / scale).astype(np.float32).astype(dtype).astype(np.float64)
    return np.moveaxis((codes * scale).reshape(v.shape), -1, axis)


WIDE = False


def mx_kscale(k):
    if not WIDE:
        return np.ones(k)
    levels = np.array([10, -10, 5, -5, 0])
    if k % 512:
        return np.exp2(np.random.permutation(np.resize(levels, k // 32))).repeat(32)
    a = np.empty((k // 512, 16))
    for p in range(k // 512):
        a[p, :8] = np.random.permutation(np.resize(levels, 8))
        for g in range(8):
            far = levels[np.abs(levels - a[p, g]) >= 10]
            a[p, g + 8] = far[np.random.randint(len(far))]
    return np.exp2(a.ravel()).repeat(32)


def f64(x):
    return np.asarray(x).astype(np.float64)


def striped(idx):
    return np.tile(idx.reshape(-1, 16).T, (8, 1)).astype(np.uint16)


def unstriped(offs):
    return offs[:16].T.reshape(-1).astype(np.int64)


E2M1 = np.array([0.0, 0.5, 1.0, 1.5, 2.0, 3.0, 4.0, 6.0, -0.0, -0.5, -1.0, -1.5, -2.0, -3.0, -4.0, -6.0])


def pack_weight(w, fmt):
    k, n = w.shape
    w = f64(np.asarray(w, np.float32).astype(ml_dtypes.bfloat16)).reshape(k // 32, 32, n)
    amax = np.abs(w).max(1)
    if fmt == "e4m3":
        byte = np.frexp(amax)[1] - 1 + 127 - 7
    else:
        mant, ex = np.frexp(amax / 6.0)
        byte = np.where(mant > 0.5, ex, ex - 1) + 127
    byte = np.clip(np.where(amax > 0, byte, 1), 1, 254)
    scaled = (w * np.exp2(127.0 - byte)[:, None, :]).reshape(k, n).astype(np.float32)
    by_word = np.ascontiguousarray(scaled.reshape(k // 512, 128, 4, n).transpose(0, 1, 3, 2))
    if fmt == "e4m3":
        words = by_word.astype(ml_dtypes.float8_e4m3fn).view(np.uint8)
    else:
        c = by_word.astype(ml_dtypes.float4_e2m1fn).view(np.uint8) & 0xF
        words = (c[..., 0::2] | (c[..., 1::2] << 4)).reshape(k // 512, 128, 2 * n)
    return np.ascontiguousarray(words), np.ascontiguousarray(byte.astype(np.uint8).reshape(k // 512, 16, n))


def unpack_weight(words, scales, fmt):
    g, _, n = scales.shape
    words = np.ascontiguousarray(words).reshape(g, 128, n, -1)
    if fmt == "e4m3":
        vals = words.view(ml_dtypes.float8_e4m3fn).astype(np.float64)
    else:
        nib = np.empty((g, 128, n, 4), np.uint8)
        nib[..., 0::2] = words & 0xF
        nib[..., 1::2] = words >> 4
        vals = E2M1[nib]
    vals = vals * np.repeat(np.exp2(scales.astype(np.float64) - 127.0), 8, axis=1)[..., None]
    return vals.transpose(0, 1, 3, 2).reshape(g * 512, n)


def pack_table(v):
    words, scales = pack_weight(v, "e4m3")
    return np.concatenate([words.reshape(words.shape[0], -1), scales.reshape(scales.shape[0], -1)], axis=1)


def unpack_table(tab):
    g, t = tab.shape[0], tab.shape[1] // 528
    return unpack_weight(tab[:, :512 * t].reshape(g, 128, t, 4), tab[:, 512 * t:].reshape(g, 16, t), "e4m3")


G, K, M, T, S = 4, 1024, 256, 4096, 512


def setup_inputs():
    n = np.random.standard_normal
    s = mx_kscale(K)[:, None]
    p_w4 = pack_weight(n((K, M)) / np.sqrt(K) / s, "e2m1")
    return {
        "tab": pack_table(n((K, T)) * s),
        "w4_words": p_w4[0],
        "w4_scales": p_w4[1],
        "dw": (0.3 * n((K, M)) / np.sqrt(K) / s).astype(np.float32),
        "r": (n((256, 512))).astype(np.float32),
        "offs": striped(np.concatenate([np.random.permutation(T)[:S] for _ in range(G)])),
    }


def reference(tab, w4_words, w4_scales, dw, r, offs):
    tab_ = unpack_table(tab)[:, unstriped(offs).reshape(G, S)].sum(1)
    w4_ = unpack_weight(w4_words, w4_scales, "e2m1")
    dw_ = mxq(f64(dw), 0, "e4m3")
    y = w4_.T @ tab_ + dw_.T @ tab_
    return f64(r) + y

@@ -1,0 +1,146 @@
+from contextlib import ExitStack
+
+import concourse.mybir as mybir
+
+G, K, M, T, S = 4, 1024, 256, 4096, 512
+P = 128
+PASSES = K // 512
+HALVES = M // P
+FLOPS = 2 * 2 * G * K * M * S
+
+F32 = mybir.dt.float32
+BF16 = mybir.dt.bfloat16
+I32 = mybir.dt.int32
+U32 = mybir.dt.uint32
+U16 = mybir.dt.uint16
+U8 = mybir.dt.uint8
+FP8X4 = mybir.dt.float8_e4m3fn_x4
+FP4X4 = mybir.dt.float4_e2m1fn_x4
+
+
+def tile_list_tabbag_sum_res_kernel(tc, tab, w4_words, w4_scales, dw, r, offs, out):
+    nc = tc.nc
+    with ExitStack() as ctx:
+        keep = ctx.enter_context(tc.tile_pool(name="keep", bufs=1))
+        psum = ctx.enter_context(tc.psum_pool(name="psum", bufs=1))
+
+        offsets = keep.tile([P, G * S // 16], U16, name="offsets")
+        nc.sync.dma_start(offsets[:], offs)
+
+        tab_scales = keep.tile([P, T], U8, name="tab_scales", align_bytes=64)
+        for a in range(PASSES):
+            rows = tab[a, 512 * T :].rearrange("(q t) -> q t", q=16)
+            nc.scalar.dma_start(tab_scales[16 * a : 16 * a + 16, :].bitcast(I32), rows.bitcast(I32))
+
+        tab_words = [keep.tile([P, T], U32, name="tab_words%d" % a, tag="words%d" % a, align_bytes=64) for a in range(PASSES)]
+        dw_raw = [keep.tile([P, 4, M], F32, name="dw_raw%d" % a) for a in range(PASSES)]
+
+        def load_words(a):
+            words = tab[a, : 512 * T].rearrange("(p b) -> p b", p=P)
+            nc.sync.dma_start(tab_words[a][:].bitcast(I32), words.bitcast(I32))
+
+        def load_dw(a):
+            rows = dw[512 * a : 512 * (a + 1), :].rearrange("(p j) n -> p j n", j=4)
+            nc.sync.dma_start(dw_raw[a][:], rows)
+
+        load_words(0)
+
+        w4_plane = keep.tile([P, PASSES, M], U8, name="w4_plane", align_bytes=64)
+        nc.vector.memset(w4_plane[:].bitcast(I32), 0)
+        nc.vector.memset(tab_scales[32:64, :].bitcast(I32), 0)
+        nc.vector.memset(tab_scales[64:128, :].bitcast(I32), 0)
+        w4_codes = keep.tile([P, PASSES, 2 * M], U8, name="w4_codes", align_bytes=64)
+        nc.scalar.dma_start(w4_codes[:].bitcast(I32), w4_words.rearrange("a p b -> p a b").bitcast(I32))
+        for q in range(4):
+            rows = w4_scales[:, 4 * q : 4 * q + 4, :].rearrange("a r n -> r a n")
+            nc.gpsimd.dma_start(w4_plane[32 * q : 32 * q + 4, :, :].bitcast(I32), rows.bitcast(I32))
+
+        load_dw(0)
+        load_words(1)
+        load_dw(1)
+
+        planes = [keep.tile([P, G * S], U8, name="plane%d" % a, align_bytes=64) for a in range(PASSES)]
+        for a in range(PASSES):
+            nc.gpsimd.memset(planes[a][:].bitcast(I32), 0)
+
+        picked_scales = keep.tile([P, G * S], U8, name="picked_scales", align_bytes=64)
+        nc.vector.tensor_copy(picked_scales[:], tab_scales[:].indirect(offsets[:]))
+        for a in range(PASSES):
+            queue = nc.scalar if a == 0 else nc.gpsimd
+            for q in range(4):
+                src = picked_scales[16 * a + 4 * q : 16 * a + 4 * q + 4, :]
+                queue.dma_start(planes[a][32 * q : 32 * q + 4, :].bitcast(I32), src.bitcast(I32))
+
+        acc = [psum.tile([P, S], F32, name="acc%d" % h) for h in range(HALVES)]
+
+        for a in range(PASSES):
+            picked = {}
+            dw_codes = {}
+            dw_plane = {}
+
+            def gather(g, tag):
+                picked[g] = keep.tile([P, S], U32, name="picked%d_%d" % (a, g), tag=tag, align_bytes=64)
+                cols = offsets[:, g * S // 16 : (g + 1) * S // 16]
+                nc.vector.tensor_copy(picked[g][:], tab_words[a][:].indirect(cols))
+
+            def quantize(h, tag):
+                grouped = keep.tile([P, P, 4], BF16, name="grouped%d_%d" % (a, h), tag=tag, align_bytes=64)
+                nc.scalar.copy(
+                    grouped[:],
+                    dw_raw[a][:, :, h * P : (h + 1) * P].rearrange("p j n -> p n j"),
+                )
+                dw_codes[h] = keep.tile([P, P], U32, name="dw_codes%d_%d" % (a, h), align_bytes=64)
+                dw_plane[h] = keep.tile([P, P], U8, name="dw_plane%d_%d" % (a, h), align_bytes=64)
+                nc.vector.quantize_mx(
+                    out=dw_codes[h][:].bitcast(FP8X4),
+                    scales=dw_plane[h][:],
+                    in_=grouped[:].rearrange("p n j -> p (n j)"),
+                )
+
+            def base(h, g):
+                nc.tensor.matmul_mx(
+                    out=acc[h][:],
+                    lhsT=w4_codes[:, a, 2 * h * P : 2 * (h + 1) * P].bitcast(FP4X4),
+                    lhsT_scale=w4_plane[:, a, h * P : (h + 1) * P],
+                    rhs=picked[g][:].bitcast(FP8X4),
+                    rhs_scale=planes[a][:, g * S : (g + 1) * S],
+                    start=(a == 0 and g == 0),
+                    stop=False,
+                )
+
+            def change(h, g):
+                nc.tensor.matmul_mx(
+                    out=acc[h][:],
+                    lhsT=dw_codes[h][:].bitcast(FP8X4),
+                    lhsT_scale=dw_plane[h][:],
+                    rhs=picked[g][:].bitcast(FP8X4),
+                    rhs_scale=planes[a][:, g * S : (g + 1) * S],
+                    start=False,
+                    stop=(a == PASSES - 1 and g == G - 1),
+                )
+
+            for g in range(2):
+                gather(g, "free%d_%d" % (a, g))
+                base(0, g)
+                base(1, g)
+            quantize(0, "hold%d_0" % a)
+            change(0, 0)
+            change(0, 1)
+            gather(2, "hold%d_0" % a)
+            base(0, 2)
+            base(1, 2)
+            change(0, 2)
+            quantize(1, "hold%d_1" % a)
+            for g in range(3):
+                change(1, g)
+            gather(3, "hold%d_1" % a)
+            for h in range(HALVES):
+                base(h, 3)
+                change(h, 3)
+
+        r_sb = keep.tile([P, HALVES, S], F32, name="r_sb", tag="words0", align_bytes=64)
+        nc.sync.dma_start(r_sb[:], r.rearrange("(h p) j -> p h j", p=P))
+        for h in range(HALVES):
+            result = keep.tile([P, S], F32, name="result%d" % h)
+            nc.vector.tensor_tensor(result[:], acc[h][:], r_sb[:, h, :], mybir.AluOpType.add)
+            nc.sync.dma_start(out[h * P : (h + 1) * P, :], result[:])

@@ -24,123 +24,134 @@ def tile_list_tabbag_sum_res_kernel(tc, tab, w4_words, w4_scales, dw, r, offs, o
         keep = ctx.enter_context(tc.tile_pool(name="keep", bufs=1))
         psum = ctx.enter_context(tc.psum_pool(name="psum", bufs=1))
 
-        offsets = keep.tile([P, G * S // 16], U16, name="offsets")
-        nc.sync.dma_start(offsets[:], offs)
+        def sbuf(shape, dtype, name, tag=None):
+            return keep.tile(shape, dtype, name=name, tag=tag or name, align_bytes=64)
 
-        tab_scales = keep.tile([P, T], U8, name="tab_scales", align_bytes=64)
-        for a in range(PASSES):
-            rows = tab[a, 512 * T :].rearrange("(q t) -> q t", q=16)
-            nc.scalar.dma_start(tab_scales[16 * a : 16 * a + 16, :].bitcast(I32), rows.bitcast(I32))
-
-        tab_words = [keep.tile([P, T], U32, name="tab_words%d" % a, tag="words%d" % a, align_bytes=64) for a in range(PASSES)]
-        dw_raw = [keep.tile([P, 4, M], F32, name="dw_raw%d" % a) for a in range(PASSES)]
-
-        def load_words(a):
-            words = tab[a, : 512 * T].rearrange("(p b) -> p b", p=P)
-            nc.sync.dma_start(tab_words[a][:].bitcast(I32), words.bitcast(I32))
-
-        def load_dw(a):
-            rows = dw[512 * a : 512 * (a + 1), :].rearrange("(p j) n -> p j n", j=4)
-            nc.sync.dma_start(dw_raw[a][:], rows)
-
-        load_words(0)
-
-        w4_plane = keep.tile([P, PASSES, M], U8, name="w4_plane", align_bytes=64)
+        w4_plane = sbuf([P, PASSES, M], U8, "w4_plane")
         nc.vector.memset(w4_plane[:].bitcast(I32), 0)
+        tab_scales = sbuf([P, T], U8, "tab_scales")
         nc.vector.memset(tab_scales[32:64, :].bitcast(I32), 0)
         nc.vector.memset(tab_scales[64:128, :].bitcast(I32), 0)
-        w4_codes = keep.tile([P, PASSES, 2 * M], U8, name="w4_codes", align_bytes=64)
-        nc.scalar.dma_start(w4_codes[:].bitcast(I32), w4_words.rearrange("a p b -> p a b").bitcast(I32))
-        for q in range(4):
+        planes = [sbuf([P, G * S], U8, "plane%d" % a) for a in range(PASSES)]
+        for a in range(PASSES):
+            nc.vector.memset(planes[a][:].bitcast(I32), 0)
+
+        def load_words(a, tag):
+            tile = sbuf([P, T], U32, "tab_words%d" % a, tag)
+            words = tab[a, : 512 * T].rearrange("(p b) -> p b", p=P)
+            nc.sync.dma_start(tile[:].bitcast(I32), words.bitcast(I32))
+            return tile
+
+        def load_dw(a, tag):
+            tile = sbuf([P, 4, M], F32, "dw_raw%d" % a, tag)
+            nc.sync.dma_start(tile[:], dw[512 * a : 512 * (a + 1), :].rearrange("(p j) n -> p j n", j=4))
+            return tile
+
+        def load_w4_scales(q):
             rows = w4_scales[:, 4 * q : 4 * q + 4, :].rearrange("a r n -> r a n")
-            nc.gpsimd.dma_start(w4_plane[32 * q : 32 * q + 4, :, :].bitcast(I32), rows.bitcast(I32))
+            nc.sync.dma_start(w4_plane[32 * q : 32 * q + 4, :, :].bitcast(I32), rows.bitcast(I32))
 
-        load_dw(0)
-        load_words(1)
-        load_dw(1)
-
-        planes = [keep.tile([P, G * S], U8, name="plane%d" % a, align_bytes=64) for a in range(PASSES)]
-        for a in range(PASSES):
-            nc.gpsimd.memset(planes[a][:].bitcast(I32), 0)
-
-        picked_scales = keep.tile([P, G * S], U8, name="picked_scales", align_bytes=64)
-        nc.vector.tensor_copy(picked_scales[:], tab_scales[:].indirect(offsets[:]))
-        for a in range(PASSES):
-            queue = nc.scalar if a == 0 else nc.gpsimd
+        def place_scales(a):
             for q in range(4):
                 src = picked_scales[16 * a + 4 * q : 16 * a + 4 * q + 4, :]
-                queue.dma_start(planes[a][32 * q : 32 * q + 4, :].bitcast(I32), src.bitcast(I32))
+                nc.sync.dma_start(planes[a][32 * q : 32 * q + 4, :].bitcast(I32), src.bitcast(I32))
+
+        offsets = keep.tile([P, G * S // 16], U16, name="offsets")
+        nc.sync.dma_start(offsets[:], offs)
+        for a in range(PASSES):
+            rows = tab[a, 512 * T :].rearrange("(q t) -> q t", q=16)
+            nc.sync.dma_start(tab_scales[16 * a : 16 * a + 16, :].bitcast(I32), rows.bitcast(I32))
+        dw_raw = {0: load_dw(0, None)}
+        w4_codes = sbuf([P, PASSES, 2 * M], U8, "w4_codes")
+        nc.sync.dma_start(w4_codes[:].bitcast(I32), w4_words.rearrange("a p b -> p a b").bitcast(I32))
+        load_w4_scales(0)
+        load_w4_scales(1)
+        tab_words = {0: load_words(0, None)}
+        load_w4_scales(2)
+        load_w4_scales(3)
+
+        picked_scales = sbuf([P, G * S], U8, "picked_scales")
+        nc.vector.tensor_copy(picked_scales[:], tab_scales[:].indirect(offsets[:]))
+        place_scales(0)
+        tab_words[1] = load_words(1, "tab_scales")
+        place_scales(1)
 
         acc = [psum.tile([P, S], F32, name="acc%d" % h) for h in range(HALVES)]
+        picked = {}
+        dw_codes = {}
+        dw_plane = {}
 
-        for a in range(PASSES):
-            picked = {}
-            dw_codes = {}
-            dw_plane = {}
+        def gather(a, g, tag):
+            picked[a, g] = sbuf([P, S], U32, "picked%d_%d" % (a, g), tag)
+            cols = offsets[:, g * S // 16 : (g + 1) * S // 16]
+            nc.vector.tensor_copy(picked[a, g][:], tab_words[a][:].indirect(cols))
 
-            def gather(g, tag):
-                picked[g] = keep.tile([P, S], U32, name="picked%d_%d" % (a, g), tag=tag, align_bytes=64)
-                cols = offsets[:, g * S // 16 : (g + 1) * S // 16]
-                nc.vector.tensor_copy(picked[g][:], tab_words[a][:].indirect(cols))
+        def quantize(a, h):
+            grouped = sbuf([P, P, 4], BF16, "grouped%d_%d" % (a, h))
+            nc.scalar.copy(grouped[:], dw_raw[a][:, :, h * P : (h + 1) * P].rearrange("p j n -> p n j"))
+            dw_codes[a, h] = sbuf([P, P], U32, "dw_codes%d_%d" % (a, h))
+            dw_plane[a, h] = sbuf([P, P], U8, "dw_plane%d_%d" % (a, h))
+            nc.vector.quantize_mx(
+                out=dw_codes[a, h][:].bitcast(FP8X4),
+                scales=dw_plane[a, h][:],
+                in_=grouped[:].rearrange("p n j -> p (n j)"),
+            )
 
-            def quantize(h, tag):
-                grouped = keep.tile([P, P, 4], BF16, name="grouped%d_%d" % (a, h), tag=tag, align_bytes=64)
-                nc.scalar.copy(
-                    grouped[:],
-                    dw_raw[a][:, :, h * P : (h + 1) * P].rearrange("p j n -> p n j"),
-                )
-                dw_codes[h] = keep.tile([P, P], U32, name="dw_codes%d_%d" % (a, h), align_bytes=64)
-                dw_plane[h] = keep.tile([P, P], U8, name="dw_plane%d_%d" % (a, h), align_bytes=64)
-                nc.vector.quantize_mx(
-                    out=dw_codes[h][:].bitcast(FP8X4),
-                    scales=dw_plane[h][:],
-                    in_=grouped[:].rearrange("p n j -> p (n j)"),
-                )
+        def base(a, h, g):
+            nc.tensor.matmul_mx(
+                out=acc[h][:],
+                lhsT=w4_codes[:, a, 2 * h * P : 2 * (h + 1) * P].bitcast(FP4X4),
+                lhsT_scale=w4_plane[:, a, h * P : (h + 1) * P],
+                rhs=picked[a, g][:].bitcast(FP8X4),
+                rhs_scale=planes[a][:, g * S : (g + 1) * S],
+                start=(a == 0 and g == 0),
+                stop=False,
+            )
 
-            def base(h, g):
-                nc.tensor.matmul_mx(
-                    out=acc[h][:],
-                    lhsT=w4_codes[:, a, 2 * h * P : 2 * (h + 1) * P].bitcast(FP4X4),
-                    lhsT_scale=w4_plane[:, a, h * P : (h + 1) * P],
-                    rhs=picked[g][:].bitcast(FP8X4),
-                    rhs_scale=planes[a][:, g * S : (g + 1) * S],
-                    start=(a == 0 and g == 0),
-                    stop=False,
-                )
+        def change(a, h, g):
+            nc.tensor.matmul_mx(
+                out=acc[h][:],
+                lhsT=dw_codes[a, h][:].bitcast(FP8X4),
+                lhsT_scale=dw_plane[a, h][:],
+                rhs=picked[a, g][:].bitcast(FP8X4),
+                rhs_scale=planes[a][:, g * S : (g + 1) * S],
+                start=False,
+                stop=(a == PASSES - 1 and g == G - 1),
+            )
 
-            def change(h, g):
-                nc.tensor.matmul_mx(
-                    out=acc[h][:],
-                    lhsT=dw_codes[h][:].bitcast(FP8X4),
-                    lhsT_scale=dw_plane[h][:],
-                    rhs=picked[g][:].bitcast(FP8X4),
-                    rhs_scale=planes[a][:, g * S : (g + 1) * S],
-                    start=False,
-                    stop=(a == PASSES - 1 and g == G - 1),
-                )
-
-            for g in range(2):
-                gather(g, "free%d_%d" % (a, g))
-                base(0, g)
-                base(1, g)
-            quantize(0, "hold%d_0" % a)
-            change(0, 0)
-            change(0, 1)
-            gather(2, "hold%d_0" % a)
-            base(0, 2)
-            base(1, 2)
-            change(0, 2)
-            quantize(1, "hold%d_1" % a)
-            for g in range(3):
-                change(1, g)
-            gather(3, "hold%d_1" % a)
-            for h in range(HALVES):
-                base(h, 3)
-                change(h, 3)
-
-        r_sb = keep.tile([P, HALVES, S], F32, name="r_sb", tag="words0", align_bytes=64)
-        nc.sync.dma_start(r_sb[:], r.rearrange("(h p) j -> p h j", p=P))
         for h in range(HALVES):
-            result = keep.tile([P, S], F32, name="result%d" % h)
+            quantize(0, h)
+        for g in range(G):
+            gather(0, g, None)
+            for h in range(HALVES):
+                base(0, h, g)
+                change(0, h, g)
+
+        dw_raw[1] = load_dw(1, "picked0_0")
+        r_sb = sbuf([P, HALVES, S], F32, "r_sb", "tab_words0")
+        nc.sync.dma_start(r_sb[:], r.rearrange("(h p) j -> p h j", p=P))
+
+        for g in range(2):
+            gather(1, g, None)
+            base(1, 0, g)
+            base(1, 1, g)
+        quantize(1, 0)
+        change(1, 0, 0)
+        change(1, 0, 1)
+        gather(1, 2, "grouped1_0")
+        base(1, 0, 2)
+        base(1, 1, 2)
+        change(1, 0, 2)
+        quantize(1, 1)
+        for g in range(3):
+            change(1, 1, g)
+        gather(1, 3, "grouped1_1")
+        for h in range(HALVES):
+            base(1, h, 3)
+            change(1, h, 3)
+
+        for h in range(HALVES):
+            result = sbuf([P, S], F32, "result%d" % h)
             nc.vector.tensor_tensor(result[:], acc[h][:], r_sb[:, h, :], mybir.AluOpType.add)
-            nc.sync.dma_start(out[h * P : (h + 1) * P, :], result[:])
+            queue = nc.sync if h == 0 else nc.scalar
+            queue.dma_start(out[h * P : (h + 1) * P, :], result[:])

@@ -6,6 +6,9 @@ G, K, M, T, S = 4, 1024, 256, 4096, 512
 P = 128
 PASSES = K // 512
 HALVES = M // P
+BLOCKS = 16
+EARLY = 1024
+AHEAD = 2
 FLOPS = 2 * 2 * G * K * M * S
 
 F32 = mybir.dt.float32
@@ -36,122 +39,108 @@ def tile_list_tabbag_sum_res_kernel(tc, tab, w4_words, w4_scales, dw, r, offs, o
         for a in range(PASSES):
             nc.vector.memset(planes[a][:].bitcast(I32), 0)
 
-        def load_words(a, tag):
-            tile = sbuf([P, T], U32, "tab_words%d" % a, tag)
-            words = tab[a, : 512 * T].rearrange("(p b) -> p b", p=P)
-            nc.sync.dma_start(tile[:].bitcast(I32), words.bitcast(I32))
-            return tile
-
-        def load_dw(a, tag):
-            tile = sbuf([P, 4, M], F32, "dw_raw%d" % a, tag)
-            nc.sync.dma_start(tile[:], dw[512 * a : 512 * (a + 1), :].rearrange("(p j) n -> p j n", j=4))
-            return tile
-
-        def load_w4_scales(q):
-            rows = w4_scales[:, 4 * q : 4 * q + 4, :].rearrange("a r n -> r a n")
-            nc.sync.dma_start(w4_plane[32 * q : 32 * q + 4, :, :].bitcast(I32), rows.bitcast(I32))
-
-        def place_scales(a):
-            for q in range(4):
-                src = picked_scales[16 * a + 4 * q : 16 * a + 4 * q + 4, :]
-                nc.sync.dma_start(planes[a][32 * q : 32 * q + 4, :].bitcast(I32), src.bitcast(I32))
-
         offsets = keep.tile([P, G * S // 16], U16, name="offsets")
+        w4_codes = sbuf([P, PASSES, 2 * M], U8, "w4_codes")
+        tab_words = [sbuf([P, T], U32, "tab_words%d" % a) for a in range(PASSES)]
+        dw_raw = [sbuf([P, 4, M], F32, "dw_raw%d" % a) for a in range(PASSES)]
+        picked_scales = sbuf([P, G * S], U8, "picked_scales")
+        r_sb = sbuf([P, HALVES, S], F32, "r_sb")
+
+        def load_words(a, t0, t1):
+            words = tab[a, : 512 * T].rearrange("(p b) -> p b", p=P).bitcast(I32)
+            nc.sync.dma_start(tab_words[a][:, t0:t1].bitcast(I32), words[:, t0:t1])
+
+        def load_dw(a):
+            nc.sync.dma_start(dw_raw[a][:], dw[512 * a : 512 * (a + 1), :].rearrange("(p i) n -> p i n", i=4))
+
+        def load_w4_scales(row):
+            rows = w4_scales[:, row:BLOCKS:4, :].rearrange("a q n -> q a n")
+            nc.sync.dma_start(w4_plane[row:P:32, :, :].bitcast(I32), rows.bitcast(I32))
+
+        def fill_plane(a):
+            for row in range(4):
+                src = picked_scales[BLOCKS * a + row : BLOCKS * (a + 1) : 4, :]
+                nc.sync.dma_start(planes[a][row:P:32, :].bitcast(I32), src.bitcast(I32))
+
         nc.sync.dma_start(offsets[:], offs)
         for a in range(PASSES):
-            rows = tab[a, 512 * T :].rearrange("(q t) -> q t", q=16)
-            nc.sync.dma_start(tab_scales[16 * a : 16 * a + 16, :].bitcast(I32), rows.bitcast(I32))
-        dw_raw = {0: load_dw(0, None)}
-        w4_codes = sbuf([P, PASSES, 2 * M], U8, "w4_codes")
+            rows = tab[a, 512 * T :].rearrange("(q t) -> q t", q=BLOCKS)
+            nc.sync.dma_start(tab_scales[BLOCKS * a : BLOCKS * (a + 1), :].bitcast(I32), rows.bitcast(I32))
         nc.sync.dma_start(w4_codes[:].bitcast(I32), w4_words.rearrange("a p b -> p a b").bitcast(I32))
-        load_w4_scales(0)
-        load_w4_scales(1)
-        tab_words = {0: load_words(0, None)}
-        load_w4_scales(2)
+        for row in range(3):
+            load_w4_scales(row)
+        load_words(0, 0, T)
         load_w4_scales(3)
-
-        picked_scales = sbuf([P, G * S], U8, "picked_scales")
+        load_dw(0)
+        load_words(1, 0, EARLY)
         nc.vector.tensor_copy(picked_scales[:], tab_scales[:].indirect(offsets[:]))
-        place_scales(0)
-        tab_words[1] = load_words(1, "tab_scales")
-        place_scales(1)
+        fill_plane(0)
+        load_words(1, EARLY, T)
+        load_dw(1)
+        fill_plane(1)
+        nc.sync.dma_start(r_sb[:], r.rearrange("(h p) j -> p h j", p=P))
 
         acc = [psum.tile([P, S], F32, name="acc%d" % h) for h in range(HALVES)]
-        picked = {}
-        dw_codes = {}
-        dw_plane = {}
 
-        def gather(a, g, tag):
-            picked[a, g] = sbuf([P, S], U32, "picked%d_%d" % (a, g), tag)
-            cols = offsets[:, g * S // 16 : (g + 1) * S // 16]
-            nc.vector.tensor_copy(picked[a, g][:], tab_words[a][:].indirect(cols))
+        def gather(a, g, tag=None):
+            picked = sbuf([P, S], U32, "picked%d_%d" % (a, g), tag)
+            nc.vector.tensor_copy(picked[:], tab_words[a][:].indirect(offsets[:, g * S // 16 : (g + 1) * S // 16]))
+            return picked
 
-        def quantize(a, h):
-            grouped = sbuf([P, P, 4], BF16, "grouped%d_%d" % (a, h))
-            nc.scalar.copy(grouped[:], dw_raw[a][:, :, h * P : (h + 1) * P].rearrange("p j n -> p n j"))
-            dw_codes[a, h] = sbuf([P, P], U32, "dw_codes%d_%d" % (a, h))
-            dw_plane[a, h] = sbuf([P, P], U8, "dw_plane%d_%d" % (a, h))
+        def quantize_dw(a):
+            grouped = sbuf([P, M, 4], BF16, "grouped%d" % a)
+            nc.scalar.copy(grouped[:], dw_raw[a][:].rearrange("p i n -> p n i"))
+            codes = sbuf([P, M], U32, "dw_codes%d" % a)
+            plane = sbuf([P, M], U8, "dw_plane%d" % a)
             nc.vector.quantize_mx(
-                out=dw_codes[a, h][:].bitcast(FP8X4),
-                scales=dw_plane[a, h][:],
-                in_=grouped[:].rearrange("p n j -> p (n j)"),
+                out=codes[:].bitcast(FP8X4),
+                scales=plane[:],
+                in_=grouped[:].rearrange("p n i -> p (n i)"),
             )
+            return codes, plane
 
-        def base(a, h, g):
+        def add_w4(a, h, g, picked):
             nc.tensor.matmul_mx(
                 out=acc[h][:],
                 lhsT=w4_codes[:, a, 2 * h * P : 2 * (h + 1) * P].bitcast(FP4X4),
                 lhsT_scale=w4_plane[:, a, h * P : (h + 1) * P],
-                rhs=picked[a, g][:].bitcast(FP8X4),
+                rhs=picked[:].bitcast(FP8X4),
                 rhs_scale=planes[a][:, g * S : (g + 1) * S],
                 start=(a == 0 and g == 0),
                 stop=False,
             )
 
-        def change(a, h, g):
+        def add_dw(a, h, g, picked, dw_mx):
+            codes, plane = dw_mx
             nc.tensor.matmul_mx(
                 out=acc[h][:],
-                lhsT=dw_codes[a, h][:].bitcast(FP8X4),
-                lhsT_scale=dw_plane[a, h][:],
-                rhs=picked[a, g][:].bitcast(FP8X4),
+                lhsT=codes[:, h * P : (h + 1) * P].bitcast(FP8X4),
+                lhsT_scale=plane[:, h * P : (h + 1) * P],
+                rhs=picked[:].bitcast(FP8X4),
                 rhs_scale=planes[a][:, g * S : (g + 1) * S],
                 start=False,
                 stop=(a == PASSES - 1 and g == G - 1),
             )
 
-        for h in range(HALVES):
-            quantize(0, h)
-        for g in range(G):
-            gather(0, g, None)
-            for h in range(HALVES):
-                base(0, h, g)
-                change(0, h, g)
+        for a in range(PASSES):
+            first = []
+            for g in range(AHEAD):
+                first.append(gather(a, g))
+                for h in range(HALVES):
+                    add_w4(a, h, g, first[g])
 
-        dw_raw[1] = load_dw(1, "picked0_0")
-        r_sb = sbuf([P, HALVES, S], F32, "r_sb", "tab_words0")
-        nc.sync.dma_start(r_sb[:], r.rearrange("(h p) j -> p h j", p=P))
+            dw_mx = quantize_dw(a)
+            for g in range(AHEAD):
+                for h in range(HALVES):
+                    add_dw(a, h, g, first[g], dw_mx)
 
-        for g in range(2):
-            gather(1, g, None)
-            base(1, 0, g)
-            base(1, 1, g)
-        quantize(1, 0)
-        change(1, 0, 0)
-        change(1, 0, 1)
-        gather(1, 2, "grouped1_0")
-        base(1, 0, 2)
-        base(1, 1, 2)
-        change(1, 0, 2)
-        quantize(1, 1)
-        for g in range(3):
-            change(1, 1, g)
-        gather(1, 3, "grouped1_1")
-        for h in range(HALVES):
-            base(1, h, 3)
-            change(1, h, 3)
+            for g, reused in zip(range(AHEAD, G), ("dw_raw%d" % a, "grouped%d" % a)):
+                picked = gather(a, g, reused)
+                for h in range(HALVES):
+                    add_w4(a, h, g, picked)
+                    add_dw(a, h, g, picked, dw_mx)
 
-        for h in range(HALVES):
-            result = sbuf([P, S], F32, "result%d" % h)
-            nc.vector.tensor_tensor(result[:], acc[h][:], r_sb[:, h, :], mybir.AluOpType.add)
-            queue = nc.sync if h == 0 else nc.scalar
-            queue.dma_start(out[h * P : (h + 1) * P, :], result[:])
+        for h, j0, j1, queue in ((0, 0, S, nc.sync), (1, 0, S // 2, nc.scalar), (1, S // 2, S, nc.sync)):
+            result = sbuf([P, j1 - j0], F32, "result%d_%d" % (h, j0))
+            nc.vector.tensor_tensor(result[:], acc[h][:, j0:j1], r_sb[:, h, j0:j1], mybir.AluOpType.add)
+            queue.dma_start(out[h * P : (h + 1) * P, j0:j1], result[:])

from contextlib import ExitStack

import concourse.mybir as mybir

G, K, M, T, S = 4, 1024, 256, 4096, 512
P = 128
PASSES = K // 512
HALVES = M // P
BLOCKS = 16
EARLY = 1024
AHEAD = 2
FLOPS = 2 * 2 * G * K * M * S

F32 = mybir.dt.float32
BF16 = mybir.dt.bfloat16
I32 = mybir.dt.int32
U32 = mybir.dt.uint32
U16 = mybir.dt.uint16
U8 = mybir.dt.uint8
FP8X4 = mybir.dt.float8_e4m3fn_x4
FP4X4 = mybir.dt.float4_e2m1fn_x4


def tile_list_tabbag_sum_res_kernel(tc, tab, w4_words, w4_scales, dw, r, offs, out):
    nc = tc.nc
    with ExitStack() as ctx:
        keep = ctx.enter_context(tc.tile_pool(name="keep", bufs=1))
        psum = ctx.enter_context(tc.psum_pool(name="psum", bufs=1))

        def sbuf(shape, dtype, name, tag=None):
            return keep.tile(shape, dtype, name=name, tag=tag or name, align_bytes=64)

        w4_plane = sbuf([P, PASSES, M], U8, "w4_plane")
        nc.vector.memset(w4_plane[:].bitcast(I32), 0)
        tab_scales = sbuf([P, T], U8, "tab_scales")
        nc.vector.memset(tab_scales[32:64, :].bitcast(I32), 0)
        nc.vector.memset(tab_scales[64:128, :].bitcast(I32), 0)
        planes = [sbuf([P, G * S], U8, "plane%d" % a) for a in range(PASSES)]
        for a in range(PASSES):
            nc.vector.memset(planes[a][:].bitcast(I32), 0)

        offsets = keep.tile([P, G * S // 16], U16, name="offsets")
        w4_codes = sbuf([P, PASSES, 2 * M], U8, "w4_codes")
        tab_words = [sbuf([P, T], U32, "tab_words%d" % a) for a in range(PASSES)]
        dw_raw = [sbuf([P, 4, M], F32, "dw_raw%d" % a) for a in range(PASSES)]
        picked_scales = sbuf([P, G * S], U8, "picked_scales")
        r_sb = sbuf([P, HALVES, S], F32, "r_sb")

        def load_words(a, t0, t1):
            words = tab[a, : 512 * T].rearrange("(p b) -> p b", p=P).bitcast(I32)
            nc.sync.dma_start(tab_words[a][:, t0:t1].bitcast(I32), words[:, t0:t1])

        def load_dw(a):
            nc.sync.dma_start(dw_raw[a][:], dw[512 * a : 512 * (a + 1), :].rearrange("(p i) n -> p i n", i=4))

        def load_w4_scales(row):
            rows = w4_scales[:, row:BLOCKS:4, :].rearrange("a q n -> q a n")
            nc.sync.dma_start(w4_plane[row:P:32, :, :].bitcast(I32), rows.bitcast(I32))

        def fill_plane(a):
            for row in range(4):
                src = picked_scales[BLOCKS * a + row : BLOCKS * (a + 1) : 4, :]
                nc.sync.dma_start(planes[a][row:P:32, :].bitcast(I32), src.bitcast(I32))

        nc.sync.dma_start(offsets[:], offs)
        for a in range(PASSES):
            rows = tab[a, 512 * T :].rearrange("(q t) -> q t", q=BLOCKS)
            nc.sync.dma_start(tab_scales[BLOCKS * a : BLOCKS * (a + 1), :].bitcast(I32), rows.bitcast(I32))
        nc.sync.dma_start(w4_codes[:].bitcast(I32), w4_words.rearrange("a p b -> p a b").bitcast(I32))
        for row in range(3):
            load_w4_scales(row)
        load_words(0, 0, T)
        load_w4_scales(3)
        load_dw(0)
        load_words(1, 0, EARLY)
        nc.vector.tensor_copy(picked_scales[:], tab_scales[:].indirect(offsets[:]))
        fill_plane(0)
        load_words(1, EARLY, T)
        load_dw(1)
        fill_plane(1)
        nc.sync.dma_start(r_sb[:], r.rearrange("(h p) j -> p h j", p=P))

        acc = [psum.tile([P, S], F32, name="acc%d" % h) for h in range(HALVES)]

        def gather(a, g, tag=None):
            picked = sbuf([P, S], U32, "picked%d_%d" % (a, g), tag)
            nc.vector.tensor_copy(picked[:], tab_words[a][:].indirect(offsets[:, g * S // 16 : (g + 1) * S // 16]))
            return picked

        def quantize_dw(a):
            grouped = sbuf([P, M, 4], BF16, "grouped%d" % a)
            nc.scalar.copy(grouped[:], dw_raw[a][:].rearrange("p i n -> p n i"))
            codes = sbuf([P, M], U32, "dw_codes%d" % a)
            plane = sbuf([P, M], U8, "dw_plane%d" % a)
            nc.vector.quantize_mx(
                out=codes[:].bitcast(FP8X4),
                scales=plane[:],
                in_=grouped[:].rearrange("p n i -> p (n i)"),
            )
            return codes, plane

        def add_w4(a, h, g, picked):
            nc.tensor.matmul_mx(
                out=acc[h][:],
                lhsT=w4_codes[:, a, 2 * h * P : 2 * (h + 1) * P].bitcast(FP4X4),
                lhsT_scale=w4_plane[:, a, h * P : (h + 1) * P],
                rhs=picked[:].bitcast(FP8X4),
                rhs_scale=planes[a][:, g * S : (g + 1) * S],
                start=(a == 0 and g == 0),
                stop=False,
            )

        def add_dw(a, h, g, picked, dw_mx):
            codes, plane = dw_mx
            nc.tensor.matmul_mx(
                out=acc[h][:],
                lhsT=codes[:, h * P : (h + 1) * P].bitcast(FP8X4),
                lhsT_scale=plane[:, h * P : (h + 1) * P],
                rhs=picked[:].bitcast(FP8X4),
                rhs_scale=planes[a][:, g * S : (g + 1) * S],
                start=False,
                stop=(a == PASSES - 1 and g == G - 1),
            )

        for a in range(PASSES):
            first = []
            for g in range(AHEAD):
                first.append(gather(a, g))
                for h in range(HALVES):
                    add_w4(a, h, g, first[g])

            dw_mx = quantize_dw(a)
            for g in range(AHEAD):
                for h in range(HALVES):
                    add_dw(a, h, g, first[g], dw_mx)

            for g, reused in zip(range(AHEAD, G), ("dw_raw%d" % a, "grouped%d" % a)):
                picked = gather(a, g, reused)
                for h in range(HALVES):
                    add_w4(a, h, g, picked)
                    add_dw(a, h, g, picked, dw_mx)

        for h, j0, j1, queue in ((0, 0, S, nc.sync), (1, 0, S // 2, nc.scalar), (1, S // 2, S, nc.sync)):
            result = sbuf([P, j1 - j0], F32, "result%d_%d" % (h, j0))
            nc.vector.tensor_tensor(result[:], acc[h][:, j0:j1], r_sb[:, h, j0:j1], mybir.AluOpType.add)
            queue.dma_start(out[h * P : (h + 1) * P, j0:j1], result[:])
